import numpy as np
import ml_dtypes


def mxq(x, axis, fmt="e4m3"):
    dtype, down = {"e4m3": (ml_dtypes.float8_e4m3fn, 7), "e5m2": (ml_dtypes.float8_e5m2, 14)}[fmt]
    v = np.moveaxis(np.asarray(x, np.float32).astype(ml_dtypes.bfloat16).astype(np.float64), axis, -1)
    blocks = v.reshape(v.shape[:-1] + (-1, 32))
    amax = np.abs(blocks).max(-1, keepdims=True)
    byte = np.maximum(np.where(amax > 0, np.frexp(amax)[1] - 1 + 127, 0) - down, 1)
    scale = np.exp2(byte - 127.0)
    codes = (blocks / scale).astype(np.float32).astype(dtype).astype(np.float64)
    return np.moveaxis((codes * scale).reshape(v.shape), -1, axis)


WIDE = False


def mx_kscale(k):
    if not WIDE:
        return np.ones(k)
    levels = np.array([30, -30])
    if k % 512:
        return np.exp2(np.random.permutation(np.resize(levels, k // 32))).repeat(32)
    a = np.empty((k // 512, 16))
    for p in range(k // 512):
        a[p, :8] = np.random.permutation(np.resize(levels, 8))
        for g in range(8):
            far = levels[np.abs(levels - a[p, g]) >= 10]
            a[p, g + 8] = far[np.random.randint(len(far))]
    return np.exp2(a.ravel()).repeat(32)


def f64(x):
    return np.asarray(x).astype(np.float64)


def striped(idx):
    return np.tile(np.asarray(idx).reshape(-1, 16).T, (8, 1)).astype(np.uint16)


def unstriped(offs):
    return offs[:16].T.reshape(-1).astype(np.int64)


E2M1 = np.array([0.0, 0.5, 1.0, 1.5, 2.0, 3.0, 4.0, 6.0, -0.0, -0.5, -1.0, -1.5, -2.0, -3.0, -4.0, -6.0])


def pack_weight(w, fmt):
    k, n = w.shape
    w = f64(np.asarray(w, np.float32).astype(ml_dtypes.bfloat16)).reshape(k // 32, 32, n)
    amax = np.abs(w).max(1)
    if fmt in ("e4m3", "e5m2"):
        byte = np.frexp(amax)[1] - 1 + 127 - (7 if fmt == "e4m3" else 14)
    else:
        mant, ex = np.frexp(amax / 6.0)
        byte = np.where(mant > 0.5, ex, ex - 1) + 127
    byte = np.clip(np.where(amax > 0, byte, 1), 1, 254)
    scaled = (w * np.exp2(127.0 - byte)[:, None, :]).reshape(k, n).astype(np.float32)
    by_word = np.ascontiguousarray(scaled.reshape(k // 512, 128, 4, n).transpose(0, 1, 3, 2))
    if fmt in ("e4m3", "e5m2"):
        words = by_word.astype(ml_dtypes.float8_e4m3fn if fmt == "e4m3" else ml_dtypes.float8_e5m2).view(np.uint8)
    else:
        c = by_word.astype(ml_dtypes.float4_e2m1fn).view(np.uint8) & 0xF
        words = (c[..., 0::2] | (c[..., 1::2] << 4)).reshape(k // 512, 128, 2 * n)
    return np.ascontiguousarray(words), np.ascontiguousarray(byte.astype(np.uint8).reshape(k // 512, 16, n))


def unpack_weight(words, scales, fmt):
    g, _, n = scales.shape
    words = np.ascontiguousarray(words).reshape(g, 128, n, -1)
    if fmt in ("e4m3", "e5m2"):
        vals = words.view(ml_dtypes.float8_e4m3fn if fmt == "e4m3" else ml_dtypes.float8_e5m2).astype(np.float64)
    else:
        nib = np.empty((g, 128, n, 4), np.uint8)
        nib[..., 0::2] = words & 0xF
        nib[..., 1::2] = words >> 4
        vals = E2M1[nib]
    vals = vals * np.repeat(np.exp2(scales.astype(np.float64) - 127.0), 8, axis=1)[..., None]
    return vals.transpose(0, 1, 3, 2).reshape(g * 512, n)


def sgn(shape):
    return np.random.uniform(0.5, 2.0, shape) * np.where(np.random.standard_normal(shape) < 0, -1.0, 1.0)


K, T, J, R, C, I, O, N = 512, 1024, 256, 512, 256, 128, 128, 256


def setup_inputs():
    n = np.random.standard_normal
    idx = np.random.permutation(T)[:J]
    idx2 = np.random.permutation(J)[:I]
    idx3 = np.random.permutation(J)[:I]
    idx4 = np.random.permutation(C)[:I]
    idx5 = np.random.permutation(C)[:O]
    fk = mx_kscale(K)
    fr = mx_kscale(R)
    xtp = pack_weight(n((K, T)) / fk[:, None], "e5m2")
    wp = pack_weight(n((K, R)) * 1 / np.sqrt(K) * fk[:, None], "e2m1")
    w2p = pack_weight(n((K, R)) * 1 / np.sqrt(K) * fk[:, None], "e4m3")
    wbp = pack_weight(n((R, N)) * 1 / np.sqrt(R) / fr[:, None], "e2m1")
    return {
        "xt_words": xtp[0],
        "xt_scales": xtp[1],
        "w_words": wp[0],
        "w_scales": wp[1],
        "w2_words": w2p[0],
        "w2_scales": w2p[1],
        "sa": (sgn((R, 1))).astype(np.float32),
        "sb": (np.random.uniform(0.5, 1.6, (R, 1)) * fr[:, None]).astype(np.float32),
        "wb_words": wbp[0],
        "wb_scales": wbp[1],
        "offs": striped(idx),
        "offs2": striped(idx2),
        "offs3": striped(idx3),
        "offs4": striped(idx4),
        "offs5": striped(idx5),
    }


def reference(xt_words, xt_scales, w_words, w_scales, w2_words, w2_scales, sa, sb, wb_words, wb_scales, offs, offs2, offs3, offs4, offs5):
    idx = unstriped(offs)
    idx2 = unstriped(offs2)
    idx3 = unstriped(offs3)
    idx4 = unstriped(offs4)
    idx5 = unstriped(offs5)
    xtu = unpack_weight(xt_words, xt_scales, "e5m2")
    wu = unpack_weight(w_words, w_scales, "e2m1")
    w2u = unpack_weight(w2_words, w2_scales, "e4m3")
    wbu = unpack_weight(wb_words, wb_scales, "e2m1")
    xtidxg = xtu[:, idx]
    a = wu.T @ xtidxg
    b = w2u.T @ xtidxg
    h1 = np.maximum(a[:, idx2] * f64(sa), b[:, idx3])
    pw = np.zeros((R, C))
    pw[:, idx4] = h1 * f64(sb)
    hid = pw[:, idx5]
    hidq = mxq(hid, 0, "e4m3")
    p = wbu.T @ hidq
    return p

@@ -1,0 +1,190 @@
+from contextlib import ExitStack
+
+import concourse.mybir as mybir
+
+K, T, J, R, C, I, O, N = 512, 1024, 256, 512, 256, 128, 128, 256
+FLOPS = 2 * K * R * J * 2 + 2 * R * N * O
+
+F32 = mybir.dt.float32
+BF16 = mybir.dt.bfloat16
+I32 = mybir.dt.int32
+U32 = mybir.dt.uint32
+U16 = mybir.dt.uint16
+U8 = mybir.dt.uint8
+E4M3X4 = mybir.dt.float8_e4m3fn_x4
+E5M2X4 = mybir.dt.float8_e5m2_x4
+E2M1X4 = mybir.dt.float4_e2m1fn_x4
+COPY = mybir.ActivationFunctionType.Copy
+MAX = mybir.AluOpType.max
+
+P = 128
+PACK = 4
+
+
+def tile_list_seatsput_kernel(tc, xt_words, xt_scales, w_words, w_scales, w2_words, w2_scales, sa, sb,
+                                  wb_words, wb_scales, offs, offs2, offs3, offs4, offs5, out):
+    nc = tc.nc
+    with ExitStack() as ctx:
+        lists = ctx.enter_context(tc.tile_pool(name="lists", bufs=1))
+        sb_pool = ctx.enter_context(tc.tile_pool(name="sbuf", bufs=1))
+        psum = ctx.enter_context(tc.psum_pool(name="psum", bufs=1))
+
+        def new(shape, dtype, name):
+            return sb_pool.tile(shape, dtype, name=name, align_bytes=64)
+
+        l1 = lists.tile([P, J // 16], U16, name="l1")
+        l2 = lists.tile([P, I // 16], U16, name="l2")
+        l3 = lists.tile([P, I // 16], U16, name="l3")
+        l4 = lists.tile([P, I // 16], U16, name="l4")
+        l5 = lists.tile([P, O // 16], U16, name="l5")
+
+        xw = new([P, T], U32, "xw")
+        xs = new([P, T], U8, "xs")
+        ww = new([P, R], U16, "ww")
+        w2w = new([P, R], U32, "w2w")
+        ws = new([P, 2 * R], U8, "ws")
+        w2s = new([P, 2 * R], U8, "w2s")
+        wbw = new([P, 2 * N], U8, "wbw")
+        wbs = new([P, N], U8, "wbs")
+        sa_t = new([P, PACK], F32, "sa_t")
+        sb_t = new([P, PACK], F32, "sb_t")
+        pw = [new([P, C], F32, "pw%d" % t) for t in range(PACK)]
+
+        for plane in (xs, ws, w2s, wbs):
+            nc.vector.memset(plane[:].bitcast(I32), 0)
+        for t in range(PACK):
+            nc.vector.memset(pw[t][:], 0.0)
+
+        def load_plane(plane, scales):
+            for q in range(4):
+                nc.sync.dma_start(out=plane[32 * q : 32 * q + 4, :].bitcast(I32), in_=scales[0, 4 * q : 4 * q + 4, :].bitcast(I32))
+
+        def load_folded(plane, scales, base):
+            rows = scales[0].bitcast(I32).rearrange("(h q r) c -> q r h c", h=2, q=2)
+            for q in range(2):
+                p0 = base + 32 * q
+                nc.sync.dma_start(out=plane[p0 : p0 + 4, :].bitcast(I32).rearrange("r (h c) -> r h c", h=2), in_=rows[q])
+
+        load_plane(xs, xt_scales)
+        nc.sync.dma_start(l1[:], offs)
+        load_folded(ws, w_scales, 0)
+        nc.sync.dma_start(out=xw[:].bitcast(I32), in_=xt_words[0].rearrange("p n t -> p (n t)").bitcast(I32))
+        nc.sync.dma_start(out=ww[:].bitcast(I32), in_=w_words[0].bitcast(I32))
+        load_folded(w2s, w2_scales, 64)
+        nc.sync.dma_start(out=w2w[:].bitcast(I32), in_=w2_words[0].rearrange("p n t -> p (n t)").bitcast(I32))
+        nc.sync.dma_start(l2[:], offs2)
+        nc.sync.dma_start(out=sa_t[:], in_=sa.rearrange("(p t) o -> p (t o)", t=PACK))
+        nc.sync.dma_start(l3[:], offs3)
+        nc.sync.dma_start(out=sb_t[:], in_=sb.rearrange("(p t) o -> p (t o)", t=PACK))
+        nc.sync.dma_start(l4[:], offs4)
+        nc.sync.dma_start(l5[:], offs5)
+        nc.sync.dma_start(out=wbw[:].bitcast(I32), in_=wb_words[0].bitcast(I32))
+        load_plane(wbs, wb_scales)
+
+        xg = new([P, J], U32, "xg")
+        xgs = new([P, J], U8, "xgs")
+        wsp = [new([P, 2, P], U8, "wsp%d" % u) for u in range(2)]
+        w2sp = [new([P, 2, P], U8, "w2sp%d" % u) for u in range(2)]
+
+        def deal_scales(dst, src, u):
+            nc.vector.tensor_copy(out=dst[u][:], in_=src.rearrange("p (m t) -> p t m", t=PACK)[:, 2 * u : 2 * u + 2, :])
+        wp = [new([P, 2, P], U16, "wp%d" % u) for u in range(2)]
+        w2p = [new([P, 2, P], U32, "w2p%d" % u) for u in range(2)]
+
+        nc.vector.tensor_copy(out=xgs[:], in_=xs[:].indirect(l1[:]))
+        nc.vector.tensor_copy(out=ws[64:128, 0:R].bitcast(I32), in_=ws[0:64, R : 2 * R].bitcast(I32))
+        deal_scales(wsp, ws[:, 0:R], 0)
+        deal_scales(wsp, ws[:, 0:R], 1)
+        nc.vector.tensor_copy(out=xg[:], in_=xw[:].indirect(l1[:]))
+        nc.vector.tensor_copy(out=w2s[0:64, R : 2 * R].bitcast(I32), in_=w2s[64:128, 0:R].bitcast(I32))
+        deal_scales(w2sp, w2s[:, R : 2 * R], 0)
+        for u in range(2):
+            nc.scalar.copy(out=wp[u][:], in_=ww[:].rearrange("p (m t) -> p t m", t=PACK)[:, 2 * u : 2 * u + 2, :])
+        for u in range(2):
+            nc.scalar.copy(out=w2p[u][:].rearrange("p t m -> p m t"), in_=w2w[:].rearrange("p (m t) -> p m t", t=PACK)[:, :, 2 * u : 2 * u + 2])
+
+        a_sb = [new([P, J], F32, "a%d" % t) for t in range(PACK)]
+        b_sb = {}
+        ga = [new([P, I], F32, "ga%d" % t) for t in range(PACK)]
+        gb = [new([P, I], F32, "gb%d" % t) for t in range(PACK)]
+        h1 = [new([P, I], F32, "h%d" % t) for t in range(PACK)]
+
+        a_ps = [psum.tile([P, J], F32, name="a_ps%d" % t) for t in range(PACK)]
+        b_ps = [psum.tile([P, J], F32, name="b_ps%d" % t) for t in range(PACK)]
+
+        def mm_a(t):
+            nc.tensor.matmul_mx(out=a_ps[t][:], lhsT=wp[t // 2][:, t % 2, :].bitcast(E2M1X4), lhsT_scale=wsp[t // 2][:, t % 2, :],
+                                rhs=xg[:].bitcast(E5M2X4), rhs_scale=xgs[:], start=True, stop=True)
+
+        def mm_b(t):
+            nc.tensor.matmul_mx(out=b_ps[t][:], lhsT=w2p[t // 2][:, t % 2, :].bitcast(E4M3X4), lhsT_scale=w2sp[t // 2][:, t % 2, :],
+                                rhs=xg[:].bitcast(E5M2X4), rhs_scale=xgs[:], start=True, stop=True)
+
+        def out_a(t):
+            if t == 3:
+                nc.scalar.copy(out=a_sb[t][:], in_=a_ps[t][:])
+            else:
+                nc.vector.tensor_copy(out=a_sb[t][:], in_=a_ps[t][:])
+
+        def out_b(t):
+            b_sb[t] = new([P, J], F32, "b%d" % (t % 2))
+            nc.vector.tensor_copy(out=b_sb[t][:], in_=b_ps[t][:])
+
+        def pick_a(t):
+            nc.scalar.activation(out=ga[t][:], in_=a_sb[t][:].indirect(l2[:]), func=COPY, scale=sa_t[:, t : t + 1])
+
+        def pick_b(t):
+            nc.vector.tensor_copy(out=gb[t][:], in_=b_sb[t][:].indirect(l3[:]))
+
+        def larger(t):
+            nc.vector.tensor_tensor(out=h1[t][:], in0=ga[t][:], in1=gb[t][:], op=MAX)
+
+        def put(t):
+            nc.scalar.activation(out=pw[t][:].indirect(l4[:]), in_=h1[t][:], func=COPY, scale=sb_t[:, t : t + 1])
+
+        def fetch(t, hid):
+            nc.scalar.activation(out=hid[:, t : PACK * O : PACK], in_=pw[t][:].indirect(l5[:]), func=COPY)
+
+        mm_a(0)
+        mm_a(1)
+        mm_b(0)
+        mm_a(2)
+        mm_a(3)
+        mm_b(1)
+        out_a(0)
+        out_a(1)
+        deal_scales(w2sp, w2s[:, R : 2 * R], 1)
+        mm_b(2)
+        mm_b(3)
+        out_b(0)
+        out_a(2)
+        pick_a(0)
+        pick_a(1)
+        out_a(3)
+        pick_a(2)
+        pick_a(3)
+        for t in range(PACK):
+            pick_b(t)
+            if t + 1 < PACK:
+                out_b(t + 1)
+            larger(t)
+            put(t)
+        hid = new([P, PACK * O], BF16, "h2")
+        for t in range(PACK):
+            fetch(t, hid)
+
+        hq = new([P, O], U32, "hq")
+        hqs = new([P, O], U8, "hqs")
+        nc.vector.quantize_mx(out=hq[:].bitcast(E4M3X4), scales=hqs[:], in_=hid[:])
+        for h in range(2):
+            o_ps = psum.tile([P, J], F32, name="a_ps%d" % h)
+            nc.tensor.matmul_mx(out=o_ps[:, 0:O], lhsT=wbw[:, 2 * h * P : 2 * (h + 1) * P].bitcast(E2M1X4),
+                                lhsT_scale=wbs[:, h * P : (h + 1) * P],
+                                rhs=hq[:].bitcast(E4M3X4), rhs_scale=hqs[:], start=True, stop=True)
+            res = new([P, O], F32, "res%d" % h)
+            if h == 0:
+                nc.vector.tensor_copy(out=res[:], in_=o_ps[:, 0:O])
+                nc.sync.dma_start(out=out[h * P : (h + 1) * P, :], in_=res[:])
+            else:
+                nc.scalar.copy(out=res[:], in_=o_ps[:, 0:O])
+                nc.scalar.dma_start(out=out[h * P : (h + 1) * P, :], in_=res[:])

@@ -43,7 +43,7 @@ def tile_list_seatsput_kernel(tc, xt_words, xt_scales, w_words, w_scales, w2_wor
         ww = new([P, R], U16, "ww")
         w2w = new([P, R], U32, "w2w")
         ws = new([P, 2 * R], U8, "ws")
-        w2s = new([P, 2 * R], U8, "w2s")
+        w2s = new([P, R], U8, "w2s")
         wbw = new([P, 2 * N], U8, "wbw")
         wbs = new([P, N], U8, "wbs")
         sa_t = new([P, PACK], F32, "sa_t")
@@ -65,13 +65,13 @@ def tile_list_seatsput_kernel(tc, xt_words, xt_scales, w_words, w_scales, w2_wor
                 p0 = base + 32 * q
                 nc.sync.dma_start(out=plane[p0 : p0 + 4, :].bitcast(I32).rearrange("r (h c) -> r h c", h=2), in_=rows[q])
 
-        load_plane(xs, xt_scales)
         nc.sync.dma_start(l1[:], offs)
-        load_folded(ws, w_scales, 0)
         nc.sync.dma_start(out=xw[:].bitcast(I32), in_=xt_words[0].rearrange("p n t -> p (n t)").bitcast(I32))
+        load_plane(xs, xt_scales)
+        load_folded(ws, w_scales, 0)
         nc.sync.dma_start(out=ww[:].bitcast(I32), in_=w_words[0].bitcast(I32))
-        load_folded(w2s, w2_scales, 64)
         nc.sync.dma_start(out=w2w[:].bitcast(I32), in_=w2_words[0].rearrange("p n t -> p (n t)").bitcast(I32))
+        load_plane(w2s, w2_scales)
         nc.sync.dma_start(l2[:], offs2)
         nc.sync.dma_start(out=sa_t[:], in_=sa.rearrange("(p t) o -> p (t o)", t=PACK))
         nc.sync.dma_start(l3[:], offs3)
@@ -89,19 +89,18 @@ def tile_list_seatsput_kernel(tc, xt_words, xt_scales, w_words, w_scales, w2_wor
         def deal_scales(dst, src, u):
             nc.vector.tensor_copy(out=dst[u][:], in_=src.rearrange("p (m t) -> p t m", t=PACK)[:, 2 * u : 2 * u + 2, :])
         wp = [new([P, 2, P], U16, "wp%d" % u) for u in range(2)]
-        w2p = [new([P, 2, P], U32, "w2p%d" % u) for u in range(2)]
+        w2p = new([P, PACK, P], U32, "w2p")
 
-        nc.vector.tensor_copy(out=xgs[:], in_=xs[:].indirect(l1[:]))
+        nc.vector.tensor_copy(out=xg[:], in_=xw[:].indirect(l1[:]))
         nc.vector.tensor_copy(out=ws[64:128, 0:R].bitcast(I32), in_=ws[0:64, R : 2 * R].bitcast(I32))
+        nc.vector.tensor_copy(out=xgs[:], in_=xs[:].indirect(l1[:]))
         deal_scales(wsp, ws[:, 0:R], 0)
         deal_scales(wsp, ws[:, 0:R], 1)
-        nc.vector.tensor_copy(out=xg[:], in_=xw[:].indirect(l1[:]))
-        nc.vector.tensor_copy(out=w2s[0:64, R : 2 * R].bitcast(I32), in_=w2s[64:128, 0:R].bitcast(I32))
-        deal_scales(w2sp, w2s[:, R : 2 * R], 0)
+        nc.vector.tensor_copy(out=w2p[:].rearrange("p t m -> p m t"), in_=w2w[:].rearrange("p (m t) -> p m t", t=PACK))
+        deal_scales(w2sp, w2s[:], 0)
+        deal_scales(w2sp, w2s[:], 1)
         for u in range(2):
             nc.scalar.copy(out=wp[u][:], in_=ww[:].rearrange("p (m t) -> p t m", t=PACK)[:, 2 * u : 2 * u + 2, :])
-        for u in range(2):
-            nc.scalar.copy(out=w2p[u][:].rearrange("p t m -> p m t"), in_=w2w[:].rearrange("p (m t) -> p m t", t=PACK)[:, :, 2 * u : 2 * u + 2])
 
         a_sb = [new([P, J], F32, "a%d" % t) for t in range(PACK)]
         b_sb = {}
@@ -117,14 +116,11 @@ def tile_list_seatsput_kernel(tc, xt_words, xt_scales, w_words, w_scales, w2_wor
                                 rhs=xg[:].bitcast(E5M2X4), rhs_scale=xgs[:], start=True, stop=True)
 
         def mm_b(t):
-            nc.tensor.matmul_mx(out=b_ps[t][:], lhsT=w2p[t // 2][:, t % 2, :].bitcast(E4M3X4), lhsT_scale=w2sp[t // 2][:, t % 2, :],
+            nc.tensor.matmul_mx(out=b_ps[t][:], lhsT=w2p[:, t, :].bitcast(E4M3X4), lhsT_scale=w2sp[t // 2][:, t % 2, :],
                                 rhs=xg[:].bitcast(E5M2X4), rhs_scale=xgs[:], start=True, stop=True)
 
         def out_a(t):
-            if t == 3:
-                nc.scalar.copy(out=a_sb[t][:], in_=a_ps[t][:])
-            else:
-                nc.vector.tensor_copy(out=a_sb[t][:], in_=a_ps[t][:])
+            nc.scalar.copy(out=a_sb[t][:], in_=a_ps[t][:])
 
         def out_b(t):
             b_sb[t] = new([P, J], F32, "b%d" % (t % 2))
@@ -145,30 +141,22 @@ def tile_list_seatsput_kernel(tc, xt_words, xt_scales, w_words, w_scales, w2_wor
         def fetch(t, hid):
             nc.scalar.activation(out=hid[:, t : PACK * O : PACK], in_=pw[t][:].indirect(l5[:]), func=COPY)
 
-        mm_a(0)
-        mm_a(1)
-        mm_b(0)
-        mm_a(2)
-        mm_a(3)
-        mm_b(1)
-        out_a(0)
-        out_a(1)
-        deal_scales(w2sp, w2s[:, R : 2 * R], 1)
-        mm_b(2)
-        mm_b(3)
+        for t in range(PACK):
+            mm_a(t)
+        for t in range(PACK):
+            mm_b(t)
+        for t in range(PACK):
+            out_a(t)
         out_b(0)
-        out_a(2)
-        pick_a(0)
-        pick_a(1)
-        out_a(3)
-        pick_a(2)
-        pick_a(3)
+        for t in range(PACK):
+            pick_a(t)
+        out_b(1)
         for t in range(PACK):
             pick_b(t)
-            if t + 1 < PACK:
-                out_b(t + 1)
             larger(t)
             put(t)
+            if t + 2 < PACK:
+                out_b(t + 2)
         hid = new([P, PACK * O], BF16, "h2")
         for t in range(PACK):
             fetch(t, hid)

@@ -50,7 +50,7 @@ def tile_list_seatsput_kernel(tc, xt_words, xt_scales, w_words, w_scales, w2_wor
         sb_t = new([P, PACK], F32, "sb_t")
         pw = [new([P, C], F32, "pw%d" % t) for t in range(PACK)]
 
-        for plane in (xs, ws, w2s, wbs):
+        for plane in (ws, xs, w2s, wbs):
             nc.vector.memset(plane[:].bitcast(I32), 0)
         for t in range(PACK):
             nc.vector.memset(pw[t][:], 0.0)
@@ -65,10 +65,10 @@ def tile_list_seatsput_kernel(tc, xt_words, xt_scales, w_words, w_scales, w2_wor
                 p0 = base + 32 * q
                 nc.sync.dma_start(out=plane[p0 : p0 + 4, :].bitcast(I32).rearrange("r (h c) -> r h c", h=2), in_=rows[q])
 
+        load_folded(ws, w_scales, 0)
         nc.sync.dma_start(l1[:], offs)
         nc.sync.dma_start(out=xw[:].bitcast(I32), in_=xt_words[0].rearrange("p n t -> p (n t)").bitcast(I32))
         load_plane(xs, xt_scales)
-        load_folded(ws, w_scales, 0)
         nc.sync.dma_start(out=ww[:].bitcast(I32), in_=w_words[0].bitcast(I32))
         nc.sync.dma_start(out=w2w[:].bitcast(I32), in_=w2_words[0].rearrange("p n t -> p (n t)").bitcast(I32))
         load_plane(w2s, w2_scales)
@@ -91,11 +91,11 @@ def tile_list_seatsput_kernel(tc, xt_words, xt_scales, w_words, w_scales, w2_wor
         wp = [new([P, 2, P], U16, "wp%d" % u) for u in range(2)]
         w2p = new([P, PACK, P], U32, "w2p")
 
-        nc.vector.tensor_copy(out=xg[:], in_=xw[:].indirect(l1[:]))
         nc.vector.tensor_copy(out=ws[64:128, 0:R].bitcast(I32), in_=ws[0:64, R : 2 * R].bitcast(I32))
-        nc.vector.tensor_copy(out=xgs[:], in_=xs[:].indirect(l1[:]))
         deal_scales(wsp, ws[:, 0:R], 0)
         deal_scales(wsp, ws[:, 0:R], 1)
+        nc.vector.tensor_copy(out=xg[:], in_=xw[:].indirect(l1[:]))
+        nc.vector.tensor_copy(out=xgs[:], in_=xs[:].indirect(l1[:]))
         nc.vector.tensor_copy(out=w2p[:].rearrange("p t m -> p m t"), in_=w2w[:].rearrange("p (m t) -> p m t", t=PACK))
         deal_scales(w2sp, w2s[:], 0)
         deal_scales(w2sp, w2s[:], 1)

@@ -66,9 +66,9 @@ def tile_list_seatsput_kernel(tc, xt_words, xt_scales, w_words, w_scales, w2_wor
                 nc.sync.dma_start(out=plane[p0 : p0 + 4, :].bitcast(I32).rearrange("r (h c) -> r h c", h=2), in_=rows[q])
 
         load_folded(ws, w_scales, 0)
+        load_plane(xs, xt_scales)
         nc.sync.dma_start(l1[:], offs)
         nc.sync.dma_start(out=xw[:].bitcast(I32), in_=xt_words[0].rearrange("p n t -> p (n t)").bitcast(I32))
-        load_plane(xs, xt_scales)
         nc.sync.dma_start(out=ww[:].bitcast(I32), in_=w_words[0].bitcast(I32))
         nc.sync.dma_start(out=w2w[:].bitcast(I32), in_=w2_words[0].rearrange("p n t -> p (n t)").bitcast(I32))
         load_plane(w2s, w2_scales)
@@ -92,10 +92,10 @@ def tile_list_seatsput_kernel(tc, xt_words, xt_scales, w_words, w_scales, w2_wor
         w2p = new([P, PACK, P], U32, "w2p")
 
         nc.vector.tensor_copy(out=ws[64:128, 0:R].bitcast(I32), in_=ws[0:64, R : 2 * R].bitcast(I32))
+        nc.vector.tensor_copy(out=xgs[:], in_=xs[:].indirect(l1[:]))
         deal_scales(wsp, ws[:, 0:R], 0)
         deal_scales(wsp, ws[:, 0:R], 1)
         nc.vector.tensor_copy(out=xg[:], in_=xw[:].indirect(l1[:]))
-        nc.vector.tensor_copy(out=xgs[:], in_=xs[:].indirect(l1[:]))
         nc.vector.tensor_copy(out=w2p[:].rearrange("p t m -> p m t"), in_=w2w[:].rearrange("p (m t) -> p m t", t=PACK))
         deal_scales(w2sp, w2s[:], 0)
         deal_scales(w2sp, w2s[:], 1)

from contextlib import ExitStack

import concourse.mybir as mybir

K, T, J, R, C, I, O, N = 512, 1024, 256, 512, 256, 128, 128, 256
FLOPS = 2 * K * R * J * 2 + 2 * R * N * O

F32 = mybir.dt.float32
BF16 = mybir.dt.bfloat16
I32 = mybir.dt.int32
U32 = mybir.dt.uint32
U16 = mybir.dt.uint16
U8 = mybir.dt.uint8
E4M3X4 = mybir.dt.float8_e4m3fn_x4
E5M2X4 = mybir.dt.float8_e5m2_x4
E2M1X4 = mybir.dt.float4_e2m1fn_x4
COPY = mybir.ActivationFunctionType.Copy
MAX = mybir.AluOpType.max

P = 128
PACK = 4


def tile_list_seatsput_kernel(tc, xt_words, xt_scales, w_words, w_scales, w2_words, w2_scales, sa, sb,
                                  wb_words, wb_scales, offs, offs2, offs3, offs4, offs5, out):
    nc = tc.nc
    with ExitStack() as ctx:
        lists = ctx.enter_context(tc.tile_pool(name="lists", bufs=1))
        sb_pool = ctx.enter_context(tc.tile_pool(name="sbuf", bufs=1))
        psum = ctx.enter_context(tc.psum_pool(name="psum", bufs=1))

        def new(shape, dtype, name):
            return sb_pool.tile(shape, dtype, name=name, align_bytes=64)

        l1 = lists.tile([P, J // 16], U16, name="l1")
        l2 = lists.tile([P, I // 16], U16, name="l2")
        l3 = lists.tile([P, I // 16], U16, name="l3")
        l4 = lists.tile([P, I // 16], U16, name="l4")
        l5 = lists.tile([P, O // 16], U16, name="l5")

        xw = new([P, T], U32, "xw")
        xs = new([P, T], U8, "xs")
        ww = new([P, R], U16, "ww")
        w2w = new([P, R], U32, "w2w")
        ws = new([P, 2 * R], U8, "ws")
        w2s = new([P, R], U8, "w2s")
        wbw = new([P, 2 * N], U8, "wbw")
        wbs = new([P, N], U8, "wbs")
        sa_t = new([P, PACK], F32, "sa_t")
        sb_t = new([P, PACK], F32, "sb_t")
        pw = [new([P, C], F32, "pw%d" % t) for t in range(PACK)]

        for plane in (ws, xs, w2s, wbs):
            nc.vector.memset(plane[:].bitcast(I32), 0)
        for t in range(PACK):
            nc.vector.memset(pw[t][:], 0.0)

        def load_plane(plane, scales):
            for q in range(4):
                nc.sync.dma_start(out=plane[32 * q : 32 * q + 4, :].bitcast(I32), in_=scales[0, 4 * q : 4 * q + 4, :].bitcast(I32))

        def load_folded(plane, scales, base):
            rows = scales[0].bitcast(I32).rearrange("(h q r) c -> q r h c", h=2, q=2)
            for q in range(2):
                p0 = base + 32 * q
                nc.sync.dma_start(out=plane[p0 : p0 + 4, :].bitcast(I32).rearrange("r (h c) -> r h c", h=2), in_=rows[q])

        load_folded(ws, w_scales, 0)
        load_plane(xs, xt_scales)
        nc.sync.dma_start(l1[:], offs)
        nc.sync.dma_start(out=xw[:].bitcast(I32), in_=xt_words[0].rearrange("p n t -> p (n t)").bitcast(I32))
        nc.sync.dma_start(out=ww[:].bitcast(I32), in_=w_words[0].bitcast(I32))
        nc.sync.dma_start(out=w2w[:].bitcast(I32), in_=w2_words[0].rearrange("p n t -> p (n t)").bitcast(I32))
        load_plane(w2s, w2_scales)
        nc.sync.dma_start(l2[:], offs2)
        nc.sync.dma_start(out=sa_t[:], in_=sa.rearrange("(p t) o -> p (t o)", t=PACK))
        nc.sync.dma_start(l3[:], offs3)
        nc.sync.dma_start(out=sb_t[:], in_=sb.rearrange("(p t) o -> p (t o)", t=PACK))
        nc.sync.dma_start(l4[:], offs4)
        nc.sync.dma_start(l5[:], offs5)
        nc.sync.dma_start(out=wbw[:].bitcast(I32), in_=wb_words[0].bitcast(I32))
        load_plane(wbs, wb_scales)

        xg = new([P, J], U32, "xg")
        xgs = new([P, J], U8, "xgs")
        wsp = [new([P, 2, P], U8, "wsp%d" % u) for u in range(2)]
        w2sp = [new([P, 2, P], U8, "w2sp%d" % u) for u in range(2)]

        def deal_scales(dst, src, u):
            nc.vector.tensor_copy(out=dst[u][:], in_=src.rearrange("p (m t) -> p t m", t=PACK)[:, 2 * u : 2 * u + 2, :])
        wp = [new([P, 2, P], U16, "wp%d" % u) for u in range(2)]
        w2p = new([P, PACK, P], U32, "w2p")

        nc.vector.tensor_copy(out=ws[64:128, 0:R].bitcast(I32), in_=ws[0:64, R : 2 * R].bitcast(I32))
        nc.vector.tensor_copy(out=xgs[:], in_=xs[:].indirect(l1[:]))
        deal_scales(wsp, ws[:, 0:R], 0)
        deal_scales(wsp, ws[:, 0:R], 1)
        nc.vector.tensor_copy(out=xg[:], in_=xw[:].indirect(l1[:]))
        nc.vector.tensor_copy(out=w2p[:].rearrange("p t m -> p m t"), in_=w2w[:].rearrange("p (m t) -> p m t", t=PACK))
        deal_scales(w2sp, w2s[:], 0)
        deal_scales(w2sp, w2s[:], 1)
        for u in range(2):
            nc.scalar.copy(out=wp[u][:], in_=ww[:].rearrange("p (m t) -> p t m", t=PACK)[:, 2 * u : 2 * u + 2, :])

        a_sb = [new([P, J], F32, "a%d" % t) for t in range(PACK)]
        b_sb = {}
        ga = [new([P, I], F32, "ga%d" % t) for t in range(PACK)]
        gb = [new([P, I], F32, "gb%d" % t) for t in range(PACK)]
        h1 = [new([P, I], F32, "h%d" % t) for t in range(PACK)]

        a_ps = [psum.tile([P, J], F32, name="a_ps%d" % t) for t in range(PACK)]
        b_ps = [psum.tile([P, J], F32, name="b_ps%d" % t) for t in range(PACK)]

        def mm_a(t):
            nc.tensor.matmul_mx(out=a_ps[t][:], lhsT=wp[t // 2][:, t % 2, :].bitcast(E2M1X4), lhsT_scale=wsp[t // 2][:, t % 2, :],
                                rhs=xg[:].bitcast(E5M2X4), rhs_scale=xgs[:], start=True, stop=True)

        def mm_b(t):
            nc.tensor.matmul_mx(out=b_ps[t][:], lhsT=w2p[:, t, :].bitcast(E4M3X4), lhsT_scale=w2sp[t // 2][:, t % 2, :],
                                rhs=xg[:].bitcast(E5M2X4), rhs_scale=xgs[:], start=True, stop=True)

        def out_a(t):
            nc.scalar.copy(out=a_sb[t][:], in_=a_ps[t][:])

        def out_b(t):
            b_sb[t] = new([P, J], F32, "b%d" % (t % 2))
            nc.vector.tensor_copy(out=b_sb[t][:], in_=b_ps[t][:])

        def pick_a(t):
            nc.scalar.activation(out=ga[t][:], in_=a_sb[t][:].indirect(l2[:]), func=COPY, scale=sa_t[:, t : t + 1])

        def pick_b(t):
            nc.vector.tensor_copy(out=gb[t][:], in_=b_sb[t][:].indirect(l3[:]))

        def larger(t):
            nc.vector.tensor_tensor(out=h1[t][:], in0=ga[t][:], in1=gb[t][:], op=MAX)

        def put(t):
            nc.scalar.activation(out=pw[t][:].indirect(l4[:]), in_=h1[t][:], func=COPY, scale=sb_t[:, t : t + 1])

        def fetch(t, hid):
            nc.scalar.activation(out=hid[:, t : PACK * O : PACK], in_=pw[t][:].indirect(l5[:]), func=COPY)

        for t in range(PACK):
            mm_a(t)
        for t in range(PACK):
            mm_b(t)
        for t in range(PACK):
            out_a(t)
        out_b(0)
        for t in range(PACK):
            pick_a(t)
        out_b(1)
        for t in range(PACK):
            pick_b(t)
            larger(t)
            put(t)
            if t + 2 < PACK:
                out_b(t + 2)
        hid = new([P, PACK * O], BF16, "h2")
        for t in range(PACK):
            fetch(t, hid)

        hq = new([P, O], U32, "hq")
        hqs = new([P, O], U8, "hqs")
        nc.vector.quantize_mx(out=hq[:].bitcast(E4M3X4), scales=hqs[:], in_=hid[:])
        for h in range(2):
            o_ps = psum.tile([P, J], F32, name="a_ps%d" % h)
            nc.tensor.matmul_mx(out=o_ps[:, 0:O], lhsT=wbw[:, 2 * h * P : 2 * (h + 1) * P].bitcast(E2M1X4),
                                lhsT_scale=wbs[:, h * P : (h + 1) * P],
                                rhs=hq[:].bitcast(E4M3X4), rhs_scale=hqs[:], start=True, stop=True)
            res = new([P, O], F32, "res%d" % h)
            if h == 0:
                nc.vector.tensor_copy(out=res[:], in_=o_ps[:, 0:O])
                nc.sync.dma_start(out=out[h * P : (h + 1) * P, :], in_=res[:])
            else:
                nc.scalar.copy(out=res[:], in_=o_ps[:, 0:O])
                nc.scalar.dma_start(out=out[h * P : (h + 1) * P, :], in_=res[:])
